import numpy as np
CORES = [16,23,24,31,64,71]
N = 6
J, Q = 1024, 4096
def entries(a): return a.T.reshape(-1)
def pack(v, P): return np.ascontiguousarray(np.asarray(v, np.int32).reshape(-1, P).T)
def split(rng, total, parts):
    c = np.sort(rng.integers(0, total + 1, parts - 1)); return np.diff(np.concatenate([[0], c, [total]]))
def lists(rng, how):
    s = np.concatenate([[0], rng.integers(1 - Q // 2, Q // 2 + 1, N - 1), [int(rng.integers(1 - Q // 2, 1))]])
    if how == "early": s[1:] = -Q; s[N] = -2 * Q
    if how == "late": s[1:] = Q; s[N] = 0
    if how == "long":
        z = int(rng.integers(1, N - 1)); s[1:z] = -rng.integers(1, Q, z - 1); s[z] = -Q; s[z + 1] = Q; s[z + 2:N] = rng.integers(1, Q, N - z - 2); s[N] = -int(rng.integers(0, Q - s[N - 1] + 1))
    if how == "sway":
        z = int(rng.integers(1, N - 2)); e = int(rng.integers(z + 1, N - 1)); s[1:] = -rng.integers(Q // 2 + 1, Q, N); s[z + 1:e + 1] = rng.integers(Q // 2 + 1, Q - 1, e - z); s[e + 1] = s[e] - Q; s[N] = s[N - 1] - Q + int(rng.integers(1, -s[N - 1]))
    tot = Q + np.diff(s)
    L = np.stack([split(rng, int(t), J) for t in tot])
    if how == "gaps":
        L = np.zeros((N, J), np.int64)
        for r in range(N): m = 1 if r & 1 else 8; L[r, 1 + rng.permutation(J - 2)[:m]] = split(rng, int(tot[r]), m)
    if how == "long":
        L = np.zeros((N, J), np.int64); L[np.arange(N), rng.integers(0, J, N)] = tot
    return {"ln": np.stack([pack(l, 16) for l in L])}
def setup_inputs(rng):
    return dict({"x": rng.standard_normal((N, 128, J), dtype=np.float32)}, **lists(rng, "uniform"))
def setup_inputs_early(rng):
    d = setup_inputs(rng); d.update(lists(rng, "early"))
    for k in ("x",): d[k] = (d[k].astype(np.float32) * 1048576.0).astype(d[k].dtype)
    return d
def setup_inputs_gaps(rng):
    d = setup_inputs(rng); d.update(lists(rng, "gaps"))
    for k in ("x",): d[k] = (d[k].astype(np.float32) * (1 / 1024.0)).astype(d[k].dtype)
    return d
def setup_inputs_late(rng):
    d = setup_inputs(rng); d.update(lists(rng, "late"))
    return d
def setup_inputs_long(rng):
    d = setup_inputs(rng); d.update(lists(rng, "long"))
    return d
def setup_inputs_sway(rng):
    d = setup_inputs(rng); d.update(lists(rng, "sway"))
    return d
def check_inputs(x):
    bad = []
    if x["ln"].min() < 0 or x["ln"].max() >= N * Q + 1: bad.append("ln out of range")
    if int(x["ln"].sum()) > N * Q: bad.append("the lengths come to more than N * Q")
    c = np.concatenate([[0], np.cumsum([int(a.sum()) for a in x["ln"]])])
    if any(c[r] < (r - 1) * Q or c[r + 1] > (r + 2) * Q for r in range(N)): bad.append("the sums of the lengths before or up to a rank leave their bounds")
    return bad
def reference(x, ln):
    got = np.concatenate([np.repeat(x[r], entries(ln[r]), axis=1) for r in range(N)], axis=1)[:, :N * Q]
    Y = np.zeros((128, N * Q), x.dtype); Y[:, :got.shape[1]] = got
    return {"y": np.stack([Y[:, Q * r:Q * r + Q] for r in range(N)])}

@@ -1,0 +1,389 @@
+from concourse.bass import DstId, RemoteDMATransfer
+from concourse.mybir import AluOpType, ActivationFunctionType
+
+N, J, Q = 6, 1024, 4096
+LC = 8
+CH = [512, 1024, 512]
+
+SCRATCH = {
+    "W": ("sbuf", [128, 3 * J + 4], "float32"),
+    "Y": ("sbuf", [128, Q], "float32"),
+    "HB": ("sbuf", [128, 512], "float32"),
+    "LNI": ("sbuf", [128, N * LC], "int32"),
+    "F": ("sbuf", [128, 1 + N * LC], "float32"),
+    "CU": ("sbuf", [128, 1 + N * LC], "float32"),
+    "ONE": ("sbuf", [128, 1 + N * LC], "float32"),
+    "CCR": ("sbuf", [128, 128], "float32"),
+    "PR": ("sbuf", [128, 128], "float32"),
+    "QR": ("sbuf", [128, 128], "float32"),
+    "RA": ("sbuf", [128, 64], "bfloat16"),
+    "RB": ("sbuf", [128, 64], "float32"),
+    "PI": ("sbuf", [128, 1], "int32"),
+    "CI": ("sbuf", [128, 1], "int32"),
+    "BI": ("sbuf", [128, 1], "int32"),
+    "PF": ("sbuf", [128, 1], "float32"),
+    "CF": ("sbuf", [128, 1], "float32"),
+    "BF": ("sbuf", [128, 1], "float32"),
+    "E63": ("sbuf", [128, 1], "float32"),
+    "E64": ("sbuf", [128, 1], "float32"),
+    "BH": ("sbuf", [128, 4], "float32"),
+    "ZF": ("sbuf", [128, 1], "float32"),
+    "X2": ("sbuf", [128, 128], "float32"),
+    "XY": ("sbuf", [128, 128], "float32"),
+    "XZ": ("sbuf", [128, 128], "float32"),
+    "XT": ("sbuf", [128, 128], "float32"),
+    "XV": ("sbuf", [128, 128], "float32"),
+    "CA": ("sbuf", [128, 512], "float16"),
+    "CB": ("sbuf", [128, 512], "float16"),
+    "EF": ("sbuf", [128, 24], "float32"),
+    "EI": ("sbuf", [128, 24], "int32"),
+    "EB": ("sbuf", [128, 24], "int32"),
+    "BB": ("sbuf", [128, 24], "float32"),
+    "U": ("sbuf", [128, 24 * 64], "bfloat16"),
+    "S": ("sbuf", [128, 24, 128], "bfloat16"),
+    "PT": ("sbuf", [128, 66], "float16"),
+    "OFF": ("sbuf", [128, 256], "uint16"),
+    "psE": ("psum", [128, 512], "float32"),
+    "psP": ("psum", [128, 512], "float32"),
+    "psO0": ("psum", [128, 512], "float32"),
+    "psO1": ("psum", [128, 512], "float32"),
+    "psO2": ("psum", [128, 512], "float32"),
+    "psO3": ("psum", [128, 512], "float32"),
+}
+SEMAPHORES = ["ldl", "ldx", "lnp", "lnu", "ln0", "ln1", "xl", "xr", "xf", "hx", "ls", "gi", "v", "s", "t", "ys"]
+
+
+def bits(m):
+    return [i for i in range(m.bit_length()) if m >> i & 1]
+
+
+def pop(m):
+    return len(bits(m))
+
+
+def part(m, i, k):
+    b = bits(m)
+    n = len(b) // k
+    return sum(1 << e for e in b[i * n:(i + 1) * n])
+
+
+def slot(r, s):
+    return J * (s - max(r - 1, 0))
+
+
+def helpers(T, topo, s, d, ncores):
+    cs, cd = T.cores[s], T.cores[d]
+    busy = set()
+    for r in range(N):
+        c = T.cores[r]
+        if topo.chip(c) == topo.chip(cs):
+            for q in (r - 1, r + 1):
+                if 0 <= q < N and topo.chip(T.cores[q]) != topo.chip(c) and topo.may_write(c, T.cores[q]):
+                    busy.add(topo.die(c))
+    return [c for c in range(ncores) if topo.chip(c) == topo.chip(cs) and c != cs and topo.may_write(c, cd)
+            and topo.die(c) not in busy]
+
+
+def rank_program(g, core, T, topo):
+    A = AluOpType
+    sem = T.sem
+    cores = list(T.cores)
+    ncores = max(cores) + topo.CORES_PER_CHIP
+    rank = T.rank_of(core)
+    local = [0]
+
+    def offmask(c):
+        return min([topo.mask(c, q) for q in cores if topo.chip(q) != topo.chip(c)])
+
+    def send(dst, out, in_, rsem, mask):
+        rid, pid, _ = topo.addr(dst)
+        g.remote_dma(out, in_, rsem, sem.ls, pid, rid, mask)
+        local[0] += pop(mask)
+
+    def fused(items):
+        tr = []
+        for dsts, in_, rsem, mask in items:
+            ids = []
+            for d, _ in dsts:
+                a = topo.addr(d)
+                ids.append(DstId(rid=a[0], pnc=a[1]))
+            tr.append(RemoteDMATransfer(dst_ids=ids, dma_engine_mask=mask, remote_sem=rsem, srcs=[in_],
+                                        dsts=[o for _, o in dsts]))
+            local[0] += pop(mask)
+        g.remote_dma_fused(tr, local_sem=sem.ls)
+
+    relay = {}
+    for s in range(N):
+        for d in (s - 1, s + 1):
+            if 0 <= d < N and not topo.may_write(cores[s], cores[d]):
+                relay[(s, d)] = helpers(T, topo, s, d, ncores)
+
+    def relay_ln(s, d, hs):
+        w = LC // len(hs)
+        a = LC * s + w * hs.index(core)
+        send(cores[d], T.LNI[:, a:a + w], T.LNI[:, a:a + w], sem.lnu, topo.mask(core, cores[d]))
+
+    if rank is None:
+        for (s, d), hs in relay.items():
+            if core in hs:
+                w = J // len(hs)
+                i = hs.index(core)
+                g.wait_ge(sem.lnp, pop(topo.mask(cores[s], core)))
+                relay_ln(s, d, hs)
+                g.wait_ge(sem.hx, pop(topo.mask(cores[s], core)) // len(hs))
+                o = slot(d, s) + w * i
+                send(cores[d], T.W[:, o:o + w], T.HB[:, 0:w], sem.xr, topo.mask(core, cores[d]))
+                g.wait_ge(sem.ls, local[0])
+        return
+
+    r = rank
+    mate = r ^ 1
+    pa, pb = min(r, mate), max(r, mate)
+    me = slot(r, r)
+    lo = max(r - 1, 0)
+    ns = min(r + 1, N - 1) - lo + 1
+    nl = min(r + 2, N)
+    off = offmask(core)
+    full = topo.mask(core, cores[mate])
+    up = full & ~off
+    mylr = [k for k in relay if k[0] == r]
+
+    def forwards(q):
+        a, b = min(q, q ^ 1), max(q, q ^ 1)
+        res = []
+        for d in range(b + 1, N):
+            who = a if topo.may_write(cores[a], cores[d]) else b
+            if who == q:
+                res.append(d)
+        return res
+
+    def pair_mask(q):
+        c = cores[q]
+        fm = topo.mask(c, cores[q ^ 1])
+        return fm if [k for k in relay if k[0] == q] else fm & ~offmask(c)
+
+    g.sync.dma_start(T.LNI[:, LC * r:LC * r + LC], T.ln[:]).then_inc(sem.ldl, 16)
+    g.scalar.dma_start(T.W[:, me:me + J], T.x[:]).then_inc(sem.ldx, 16)
+
+    gi = [0]
+
+    def iota(out, pat, base, cm, small=True):
+        if small:
+            g.iota(out, pat, base, cm, allow_small_or_imprecise_dtypes=True).then_inc(sem.gi, 1)
+        else:
+            g.iota(out, pat, base, cm).then_inc(sem.gi, 1)
+        gi[0] += 1
+
+    iota(T.PI[:], [[0, 1]], 0, 1, False)
+    iota(T.CCR[:], [[0, 16], [1, 8]], 0, 0)
+    iota(T.PR[:], [[1, 128]], 0, 0)
+    iota(T.QR[:], [[0, 8], [1, 16]], 0, 0)
+    iota(T.RA[:], [[64, 64]], 64, 0)
+    iota(T.RB[:], [[1, 64]], 0, 0)
+
+    own = T.LNI[:, LC * r:LC * r + LC]
+    g.wait_ge(sem.ldl, 16)
+    if mylr:
+        hs = [h for h in relay[mylr[0]] if h != cores[mate]]
+        fused([([(h, own) for h in [cores[mate]] + hs], own, sem.lnp, full)])
+    else:
+        send(cores[mate], own, own, sem.lnp, pair_mask(r))
+    fw = forwards(r)
+    if fw:
+        g.wait_ge(sem.lnp, pop(pair_mask(mate)))
+        both = T.LNI[:, LC * pa:LC * pb + LC]
+        fused([([(cores[d], both) for d in fw], both, sem["ln%d" % (pa // 2)], off)])
+    carry = [(k, hs) for k, hs in relay.items() if core in hs]
+    for (s, d), hs in carry:
+        g.wait_ge(sem.lnp, pop(pair_mask(mate)))
+        relay_ln(s, d, hs)
+
+    g.wait_ge(sem.ldx, 16)
+    mt = slot(mate, r)
+    msem = sem.xl if mate > r else sem.xr
+    nxt = [d for d in (r - 1, r + 1) if 0 <= d < N and d != mate]
+    if mylr:
+        hs = relay[mylr[0]]
+        w = J // len(hs)
+        items = []
+        rest = J
+        for i, h in enumerate(hs):
+            m = part(full, i, len(hs))
+            src = T.W[:, me + w * i:me + w * i + w]
+            if h == cores[mate]:
+                items.append(([(h, T.W[:, mt + w * i:mt + w * i + w])], src, sem.xf, m))
+                rest = w * i
+            else:
+                items.append(([(h, T.HB[:, 0:w])], src, sem.hx, m))
+        fused(items)
+        send(cores[mate], T.W[:, mt:mt + rest], T.W[:, me:me + rest], msem, full)
+    elif nxt:
+        d = nxt[0]
+        od = slot(d, r)
+        fused([([(cores[d], T.W[:, od:od + J])], T.W[:, me:me + J], sem.xl if d > r else sem.xr, off),
+               ([(cores[mate], T.W[:, mt:mt + J])], T.W[:, me:me + J], msem, up)])
+    else:
+        send(cores[mate], T.W[:, mt:mt + J], T.W[:, me:me + J], msem, up if carry else full)
+    for (s, d), hs in carry:
+        w = J // len(hs)
+        i = hs.index(core)
+        a, o = slot(r, s) + w * i, slot(d, s) + w * i
+        g.wait_ge(sem.xf, pop(topo.mask(cores[s], core)) // len(hs))
+        send(cores[d], T.W[:, o:o + w], T.W[:, a:a + w], sem.xr, topo.mask(core, cores[d]))
+    g.wait_ge(sem.ls, local[0])
+
+    def xcount(s):
+        nm = sem.xl if s < r else sem.xr
+        if (s, r) in relay:
+            return [(nm, sum(pop(topo.mask(h, core)) for h in relay[(s, r)]))]
+        c = cores[s]
+        fm = topo.mask(c, core)
+        if topo.chip(c) != topo.chip(core):
+            return [(nm, pop(fm))]
+        mine = [k for k in relay if k[0] == s]
+        if mine:
+            res = [(nm, pop(fm))]
+            hs = relay[mine[0]]
+            if core in hs:
+                res.append((sem.xf, pop(fm) // len(hs)))
+            return res
+        reach = [q for q in (s - 1, s + 1) if 0 <= q < N and q != r]
+        carries = [1 for hs in relay.values() if c in hs]
+        if reach or carries:
+            return [(nm, pop(fm & ~offmask(c)))]
+        return [(nm, pop(fm))]
+
+    xwaits = [(sem.ldx, 16)]
+    for s in (r - 1, r + 1):
+        if 0 <= s < N:
+            xwaits += xcount(s)
+    lwaits = [(sem.ldl, 16), (sem.lnp, pop(pair_mask(mate)))]
+    if (r + 1, r) in relay:
+        lwaits.append((sem.lnu, sum(pop(topo.mask(h, core)) for h in relay[(r + 1, r)])))
+    elif r + 1 < N and r + 1 != mate:
+        lwaits = lwaits
+    for p in range(pa // 2):
+        who = [q for q in (2 * p, 2 * p + 1) if r in forwards(q)][0]
+        lwaits.append((sem["ln%d" % p], pop(offmask(cores[who]))))
+
+    V, SC, PE = g.vector, g.scalar, g.tensor
+    nv, nsc, nt = [0], [0], [0]
+
+    def v(ins):
+        ins.then_inc(sem.v, 1)
+        nv[0] += 1
+        return nv[0]
+
+    def sc(ins):
+        ins.then_inc(sem.s, 1)
+        nsc[0] += 1
+        return nsc[0]
+
+    def t(ins):
+        ins.then_inc(sem.t, 1)
+        nt[0] += 1
+        return nt[0]
+
+    nb = 8 * ns
+    hb = nb // 2
+    nc = nl * LC
+    o = 1 + LC * lo
+    zc = ns * J
+    v(V.memset(T.ONE[:, 0:nc + 1], 1.0))
+    v(V.memset(T.F[:, 0:1], 0.0))
+    v(V.memset(T.ZF[:], 0.0))
+    v(V.memset(T.W[:, zc:zc + 4], 0.0))
+    V.wait_ge(sem.gi, gi[0])
+    v(V.tensor_copy(T.PF[:], T.PI[:]))
+    v(V.tensor_scalar(T.CI[:], T.PI[:], 7, None, A.bitwise_and))
+    k = v(V.tensor_scalar(T.BI[:], T.PI[:], 63, None, A.bitwise_and))
+    V.wait_ge(sem.v, k)
+    v(V.tensor_copy(T.CF[:], T.CI[:]))
+    v(V.tensor_copy(T.PT[:, 0:1], T.ZF[:]))
+    k = v(V.tensor_copy(T.BF[:], T.BI[:]))
+    V.wait_ge(sem.v, k)
+    v(V.tensor_scalar(T.XZ[:], T.CCR[:], T.CF[:], None, A.is_equal))
+    k = v(V.tensor_scalar(T.XT[:], T.PR[:], T.PF[:], None, A.is_ge))
+    v(V.tensor_scalar(T.X2[:], T.CCR[:], T.CF[:], None, A.is_gt))
+    v(V.tensor_scalar(T.XY[:], T.CCR[:], T.CF[:], None, A.is_lt))
+    V.wait_ge(sem.v, k)
+    v(V.tensor_tensor(T.XV[:], T.XZ[:], T.XT[:], A.mult))
+    v(V.tensor_scalar(T.E63[:], T.BF[:], 63.0, None, A.is_equal))
+    v(V.tensor_scalar(T.E64[:], T.BF[:], 63.0, 1.0, A.is_equal, A.subtract))
+    for h in range(4):
+        k = v(V.tensor_scalar(T.BH[:, h:h + 1], T.BF[:], 16.0 * h, None, A.subtract))
+    v(V.memset(T.S[:, 0:hb, 64:128], 0.0))
+    v(V.memset(T.S[:, hb:nb, 0:64], 0.0))
+    V.wait_ge(sem.v, k)
+    for h in range(4):
+        cs = slice(128 * h, 128 * h + 128)
+        v(V.tensor_scalar(T.CA[:, cs], T.QR[:], T.BH[:, h:h + 1], T.E63[:], A.is_equal, A.add))
+        v(V.tensor_scalar(T.CB[:, cs], T.QR[:], T.BH[:, h:h + 1], T.E64[:], A.not_equal, A.add))
+
+    for q, n in lwaits:
+        V.wait_ge(q, n)
+    vf = v(V.tensor_copy(T.F[:, 1:nc + 1], T.LNI[:, 0:nc]))
+    V.wait_ge(sem.v, vf)
+    vs = v(V.tensor_tensor_scan(T.CU[:, 0:nc + 1], T.ONE[:, 0:nc + 1], T.F[:, 0:nc + 1], -32.0 * r, A.mult, A.add))
+    PE.wait_ge(sem.v, vf)
+    EA, EO = T.psE[:, 0:nb], T.psE[:, 32:32 + ns]
+    t(PE.matmul(EA, T.XV[:], T.F[:, o:o + nb], True, False))
+    PE.wait_ge(sem.v, vs)
+    t(PE.matmul(EA, T.XZ[:], T.CU[:, o - 1:o - 1 + nb], False, True))
+    t(PE.matmul(EO, T.XY[:], T.CU[:, o - 1:o - 1 + nb:8], True, False))
+    ke = t(PE.matmul(EO, T.X2[:], T.CU[:, o + 7:o + 7 + 8 * ns - 7:8], False, True))
+    V.wait_ge(sem.t, ke)
+    for i in range(ns):
+        k = v(V.tensor_scalar(T.EF[:, 8 * i:8 * i + 8], T.psE[:, 8 * i:8 * i + 8], T.psE[:, 32 + i:33 + i], 0.0,
+                              A.add, A.max))
+    V.wait_ge(sem.v, k)
+    k = v(V.tensor_copy(T.EI[:, 0:nb], T.EF[:, 0:nb]))
+    V.wait_ge(sem.v, k)
+    k = v(V.tensor_scalar(T.EB[:, 0:nb], T.EI[:, 0:nb], 63, None, A.bitwise_and))
+    V.wait_ge(sem.v, k)
+    kb = v(V.tensor_scalar(T.BB[:, 0:nb], T.EB[:, 0:nb], -1.0, 0.5, A.mult, A.add))
+
+    ku, ks = [], []
+    for b in range(nb):
+        ku.append(v(V.tensor_scalar(T.U[:, 64 * b:64 * b + 64], T.RA[:], T.EF[:, b:b + 1], None, A.is_gt)))
+    SC.wait_ge(sem.gi, gi[0])
+    SC.wait_ge(sem.v, kb)
+    for b in range(nb):
+        c0 = 0 if b < hb else 64
+        ks.append(sc(SC.activation(T.S[:, b, c0:c0 + 64], T.RB[:], ActivationFunctionType.Sign,
+                                   bias=T.BB[:, b:b + 1], scale=1.0)))
+    for b in range(0, nb, 2):
+        PE.wait_ge(sem.v, ku[b + 1])
+        PE.wait_ge(sem.s, ks[b + 1])
+        for e in (b, b + 1):
+            kp = t(PE.matmul(T.psP[:, 0:64], T.S[:, e, :], T.U[:, 64 * e:64 * e + 64], e == 0, e == nb - 1))
+    V.wait_ge(sem.t, kp)
+    k = v(V.tensor_copy(T.PT[:, 1:65], T.psP[:, 0:64]))
+    PE.wait_ge(sem.v, k)
+    for h in range(4):
+        cs = slice(128 * h, 128 * h + 128)
+        po = T["psO%d" % h]
+        t(PE.matmul(po[:, 0:64], T.CA[:, cs], T.PT[:, 1:65], True, False))
+        k = t(PE.matmul(po[:, 0:64], T.CB[:, cs], T.PT[:, 0:64], False, True))
+        V.wait_ge(sem.t, k)
+        vo = v(V.tensor_scalar(T.OFF[:, h:256:4], po[:, 0:64], 0.5, None, A.mult))
+
+    for q, n in xwaits:
+        V.wait_ge(q, n)
+        SC.wait_ge(q, n)
+    V.wait_ge(sem.v, vo)
+    SC.wait_ge(sem.v, vo)
+    win = T.W[:, 0:zc + 4]
+    c = 0
+    order = []
+    for w in CH:
+        d = c + Q // 2
+        kv = v(V.tensor_copy(T.Y[:, c:c + w], win.indirect(T.OFF[:, c // 16:(c + w) // 16])))
+        k2 = sc(SC.activation(T.Y[:, d:d + w], win.indirect(T.OFF[:, d // 16:(d + w) // 16]),
+                              ActivationFunctionType.Copy))
+        order += [(sem.v, kv, c, w), (sem.s, k2, d, w)]
+        c += w
+    for q, n, c, w in order:
+        g.sync.wait_ge(q, n)
+        g.sync.dma_start(T.y[:, c:c + w], T.Y[:, c:c + w]).then_inc(sem.ys, 16)
+    g.sync.wait_ge(sem.ys, 16 * len(order))

@@ -2,55 +2,31 @@ from concourse.bass import DstId, RemoteDMATransfer
 from concourse.mybir import AluOpType, ActivationFunctionType
 
 N, J, Q = 6, 1024, 4096
+H = J // 2
 LC = 8
-CH = [512, 1024, 512]
+CH = [384, 1024, 640]
+R = 64
+AW = Q // R
+NH = R // 16
+US = AW + 2
 
-SCRATCH = {
-    "W": ("sbuf", [128, 3 * J + 4], "float32"),
-    "Y": ("sbuf", [128, Q], "float32"),
-    "HB": ("sbuf", [128, 512], "float32"),
-    "LNI": ("sbuf", [128, N * LC], "int32"),
-    "F": ("sbuf", [128, 1 + N * LC], "float32"),
-    "CU": ("sbuf", [128, 1 + N * LC], "float32"),
-    "ONE": ("sbuf", [128, 1 + N * LC], "float32"),
-    "CCR": ("sbuf", [128, 128], "float32"),
-    "PR": ("sbuf", [128, 128], "float32"),
-    "QR": ("sbuf", [128, 128], "float32"),
-    "RA": ("sbuf", [128, 64], "bfloat16"),
-    "RB": ("sbuf", [128, 64], "float32"),
-    "PI": ("sbuf", [128, 1], "int32"),
-    "CI": ("sbuf", [128, 1], "int32"),
-    "BI": ("sbuf", [128, 1], "int32"),
-    "PF": ("sbuf", [128, 1], "float32"),
-    "CF": ("sbuf", [128, 1], "float32"),
-    "BF": ("sbuf", [128, 1], "float32"),
-    "E63": ("sbuf", [128, 1], "float32"),
-    "E64": ("sbuf", [128, 1], "float32"),
-    "BH": ("sbuf", [128, 4], "float32"),
-    "ZF": ("sbuf", [128, 1], "float32"),
-    "X2": ("sbuf", [128, 128], "float32"),
-    "XY": ("sbuf", [128, 128], "float32"),
-    "XZ": ("sbuf", [128, 128], "float32"),
-    "XT": ("sbuf", [128, 128], "float32"),
-    "XV": ("sbuf", [128, 128], "float32"),
-    "CA": ("sbuf", [128, 512], "float16"),
-    "CB": ("sbuf", [128, 512], "float16"),
-    "EF": ("sbuf", [128, 24], "float32"),
-    "EI": ("sbuf", [128, 24], "int32"),
-    "EB": ("sbuf", [128, 24], "int32"),
-    "BB": ("sbuf", [128, 24], "float32"),
-    "U": ("sbuf", [128, 24 * 64], "bfloat16"),
-    "S": ("sbuf", [128, 24, 128], "bfloat16"),
-    "PT": ("sbuf", [128, 66], "float16"),
+SCRATCH = {k: ("sbuf", [128, n], "int32") for k, n in
+           {"LNI": 48, "PI": 1, "CI": 1, "BI": 1, "EI": 24, "EB": 24}.items()}
+SCRATCH.update({k: ("sbuf", [128, n], "float32") for k, n in {
+    "W": 3 * J + 4, "Y": Q, "HB": H, "F": 24, "CU": 49, "ONE": 49, "CCR": 128, "PR": 128, "QR": 128,
+    "PF": 1, "CF": 1, "BF": 1, "EL": 1, "EM": 1, "BH": NH, "X2": 128, "XY": 128, "XZ": 128, "XT": 128,
+    "XV": 128, "EF": 24, "BB": 24}.items()})
+SCRATCH.update({
+    "RA": ("sbuf", [128, US], "bfloat16"),
+    "CA": ("sbuf", [128, 128 * NH], "float16"),
+    "CB": ("sbuf", [128, 128 * NH], "float16"),
+    "U": ("sbuf", [128, 24 * US], "bfloat16"),
+    "S": ("sbuf", [128, 24, 2 * R], "bfloat16"),
+    "PT": ("sbuf", [128, US], "float16"),
     "OFF": ("sbuf", [128, 256], "uint16"),
-    "psE": ("psum", [128, 512], "float32"),
-    "psP": ("psum", [128, 512], "float32"),
-    "psO0": ("psum", [128, 512], "float32"),
-    "psO1": ("psum", [128, 512], "float32"),
-    "psO2": ("psum", [128, 512], "float32"),
-    "psO3": ("psum", [128, 512], "float32"),
-}
-SEMAPHORES = ["ldl", "ldx", "lnp", "lnu", "ln0", "ln1", "xl", "xr", "xf", "hx", "ls", "gi", "v", "s", "t", "ys"]
+})
+SCRATCH.update({k: ("psum", [128, 512], "float32") for k in ["psE", "psP"] + ["psO%d" % h for h in range(NH)]})
+SEMAPHORES = ["ldl", "ldx", "ldy", "lnp", "lnu", "ln0", "ln1", "xl", "xr", "xf", "hx", "ls", "gi", "v", "s", "t", "ys"]
 
 
 def bits(m):
@@ -71,29 +47,53 @@ def slot(r, s):
     return J * (s - max(r - 1, 0))
 
 
-def helpers(T, topo, s, d, ncores):
-    cs, cd = T.cores[s], T.cores[d]
-    busy = set()
-    for r in range(N):
-        c = T.cores[r]
-        if topo.chip(c) == topo.chip(cs):
-            for q in (r - 1, r + 1):
-                if 0 <= q < N and topo.chip(T.cores[q]) != topo.chip(c) and topo.may_write(c, T.cores[q]):
-                    busy.add(topo.die(c))
-    return [c for c in range(ncores) if topo.chip(c) == topo.chip(cs) and c != cs and topo.may_write(c, cd)
-            and topo.die(c) not in busy]
+def plan(cores, topo):
+    ncores = max(cores) + topo.CORES_PER_CHIP
+    pairs = [(s, d) for s in range(N) for d in (s - 1, s + 1)
+             if 0 <= d < N and topo.chip(cores[s]) != topo.chip(cores[d])]
+    half, relay, used = {}, {}, set()
+
+    def ports(s, d):
+        return [c for c in range(ncores) if topo.chip(c) == topo.chip(cores[s]) and c != cores[s]
+                and topo.may_write(c, cores[d]) and c not in used]
+
+    for s, d in pairs:
+        if topo.may_write(cores[s], cores[d]):
+            c = [c for c in ports(s, d) if c not in cores and topo.die(c) != topo.die(cores[s])][-1]
+            half[s] = (c, d)
+            used.update((c, cores[s]))
+    for s, d in pairs:
+        if not topo.may_write(cores[s], cores[d]):
+            hs = ports(s, d)
+            near = [c for c in hs if topo.die(c) == topo.die(cores[s])]
+            far = [c for c in hs if topo.die(c) != topo.die(cores[s])]
+            phases = [far, near] if len(hs) == 2 else [near, far]
+            res, o = [], 0
+            for ph, cs in enumerate(phases):
+                for i, c in enumerate(cs):
+                    w = H // len(cs)
+                    ln = (LC // 2 * ph, LC // 2 * ph + LC // 2) if i == 0 else None
+                    too = len(cs) == 1 and c not in cores and topo.die(c) == topo.die(cores[s ^ 1])
+                    res.append((c, o, w, ph, part(topo.mask(cores[s], c), i, len(cs)), ln, too))
+                    o += w
+            relay[(s, d)] = res
+    return half, relay
 
 
 def rank_program(g, core, T, topo):
     A = AluOpType
     sem = T.sem
     cores = list(T.cores)
-    ncores = max(cores) + topo.CORES_PER_CHIP
     rank = T.rank_of(core)
     local = [0]
+    half, relay = plan(cores, topo)
+    own_relay = {k[0]: (k[1], hs) for k, hs in relay.items()}
 
     def offmask(c):
         return min([topo.mask(c, q) for q in cores if topo.chip(q) != topo.chip(c)])
+
+    def upper(c, d):
+        return topo.mask(c, d) & ~offmask(c)
 
     def send(dst, out, in_, rsem, mask):
         rid, pid, _ = topo.addr(dst)
@@ -112,159 +112,141 @@ def rank_program(g, core, T, topo):
             local[0] += pop(mask)
         g.remote_dma_fused(tr, local_sem=sem.ls)
 
-    relay = {}
-    for s in range(N):
-        for d in (s - 1, s + 1):
-            if 0 <= d < N and not topo.may_write(cores[s], cores[d]):
-                relay[(s, d)] = helpers(T, topo, s, d, ncores)
+    def xsem(d, s):
+        return sem.xl if s < d else sem.xr
 
-    def relay_ln(s, d, hs):
-        w = LC // len(hs)
-        a = LC * s + w * hs.index(core)
-        send(cores[d], T.LNI[:, a:a + w], T.LNI[:, a:a + w], sem.lnu, topo.mask(core, cores[d]))
+    def wx(d, s, a, w):
+        return T.W[:, slot(d, s) + a:slot(d, s) + a + w]
+
+    def pair_mask(q):
+        return topo.mask(cores[q], cores[q ^ 1]) if q in own_relay else upper(cores[q], cores[q ^ 1])
+
+    def forwards(q):
+        a, b = min(q, q ^ 1), max(q, q ^ 1)
+        return [d for d in range(b + 1, N) if (a if topo.may_write(cores[a], cores[d]) else b) == q]
+
+    def both_lists(q):
+        a = LC * min(q, q ^ 1)
+        return T.LNI[:, a:a + 2 * LC]
+
+    def to_both(s, src, a, w):
+        d, m = half[s][1], s ^ 1
+        fused([([(cores[d], wx(d, s, a, w))], src, xsem(d, s), offmask(core)),
+               ([(cores[m], wx(m, s, a, w))], src, xsem(m, s), upper(core, cores[m]))])
 
     if rank is None:
-        for (s, d), hs in relay.items():
-            if core in hs:
-                w = J // len(hs)
-                i = hs.index(core)
-                g.wait_ge(sem.lnp, pop(topo.mask(cores[s], core)))
-                relay_ln(s, d, hs)
-                g.wait_ge(sem.hx, pop(topo.mask(cores[s], core)) // len(hs))
-                o = slot(d, s) + w * i
-                send(cores[d], T.W[:, o:o + w], T.HB[:, 0:w], sem.xr, topo.mask(core, cores[d]))
+        for s, (c, d) in half.items():
+            if c == core:
+                g.wait_ge(sem.lnp, pop(pair_mask(s)) + pop(pair_mask(s ^ 1)))
+                fw = forwards(s)[1:]
+                both = both_lists(s)
+                fused([([(cores[q], both) for q in fw], both, sem["ln%d" % (s // 2)], offmask(core))])
+                g.wait_ge(sem.hx, pop(topo.mask(cores[s], core)))
+                to_both(s, T.HB[:], 0, H)
                 g.wait_ge(sem.ls, local[0])
+        for (s, d), hs in relay.items():
+            for c, o, w, ph, m, ln, too in hs:
+                if c == core:
+                    if ln:
+                        a = T.LNI[:, LC * s + ln[0]:LC * s + ln[1]]
+                        g.wait_ge(sem.lnp, pop(pair_mask(s)))
+                        send(cores[d], a, a, sem.lnu, offmask(core))
+                    g.wait_ge(sem.hx, pop(m))
+                    src = T.HB[:, 0:w]
+                    if too:
+                        q = s ^ 1
+                        fused([([(cores[d], wx(d, s, o, w))], src, xsem(d, s), offmask(core)),
+                               ([(cores[q], wx(q, s, o, w))], src, xsem(q, s), upper(core, cores[q]))])
+                    else:
+                        send(cores[d], wx(d, s, o, w), src, xsem(d, s), offmask(core))
+                    g.wait_ge(sem.ls, local[0])
         return
 
     r = rank
     mate = r ^ 1
-    pa, pb = min(r, mate), max(r, mate)
     me = slot(r, r)
     lo = max(r - 1, 0)
     ns = min(r + 1, N - 1) - lo + 1
     nl = min(r + 2, N)
-    off = offmask(core)
     full = topo.mask(core, cores[mate])
-    up = full & ~off
-    mylr = [k for k in relay if k[0] == r]
-
-    def forwards(q):
-        a, b = min(q, q ^ 1), max(q, q ^ 1)
-        res = []
-        for d in range(b + 1, N):
-            who = a if topo.may_write(cores[a], cores[d]) else b
-            if who == q:
-                res.append(d)
-        return res
-
-    def pair_mask(q):
-        c = cores[q]
-        fm = topo.mask(c, cores[q ^ 1])
-        return fm if [k for k in relay if k[0] == q] else fm & ~offmask(c)
-
-    g.sync.dma_start(T.LNI[:, LC * r:LC * r + LC], T.ln[:]).then_inc(sem.ldl, 16)
-    g.scalar.dma_start(T.W[:, me:me + J], T.x[:]).then_inc(sem.ldx, 16)
-
-    gi = [0]
-
-    def iota(out, pat, base, cm, small=True):
-        if small:
-            g.iota(out, pat, base, cm, allow_small_or_imprecise_dtypes=True).then_inc(sem.gi, 1)
-        else:
-            g.iota(out, pat, base, cm).then_inc(sem.gi, 1)
-        gi[0] += 1
-
-    iota(T.PI[:], [[0, 1]], 0, 1, False)
-    iota(T.CCR[:], [[0, 16], [1, 8]], 0, 0)
-    iota(T.PR[:], [[1, 128]], 0, 0)
-    iota(T.QR[:], [[0, 8], [1, 16]], 0, 0)
-    iota(T.RA[:], [[64, 64]], 64, 0)
-    iota(T.RB[:], [[1, 64]], 0, 0)
 
     own = T.LNI[:, LC * r:LC * r + LC]
+    g.sync.dma_start(own, T.ln[:]).then_inc(sem.ldl, 16)
+    g.sync.dma_start(T.W[:, me:me + H], T.x[:, 0:H]).then_inc(sem.ldx, 16)
+    g.sync.dma_start(T.W[:, me + H:me + J], T.x[:, H:J]).then_inc(sem.ldy, 16)
+
+    g.iota(T.PI[:], [[0, 1]], 0, 1).then_inc(sem.gi, 1)
+    for buf, pat in ((T.CCR, [[0, 16], [1, 8]]), (T.PR, [[1, 128]]), (T.QR, [[0, 8], [1, 16]])):
+        g.iota(buf[:], pat, 0, 0, allow_small_or_imprecise_dtypes=True).then_inc(sem.gi, 1)
+
     g.wait_ge(sem.ldl, 16)
-    if mylr:
-        hs = [h for h in relay[mylr[0]] if h != cores[mate]]
-        fused([([(h, own) for h in [cores[mate]] + hs], own, sem.lnp, full)])
-    else:
-        send(cores[mate], own, own, sem.lnp, pair_mask(r))
-    fw = forwards(r)
+    dsts = []
+    if r in own_relay:
+        dsts += [e[0] for e in own_relay[r][1] if e[5]]
+    dsts += [half[q][0] for q in (r, mate) if q in half]
+    dsts.append(cores[mate])
+    fused([([(c, own) for c in dsts], own, sem.lnp, pair_mask(r))])
+    if r in half:
+        g.wait_ge(sem.ldx, 16)
+        send(half[r][0], T.HB[:], wx(r, r, 0, H), sem.hx, topo.mask(core, half[r][0]))
+    fw = forwards(r)[:1] if r in half else forwards(r)
     if fw:
         g.wait_ge(sem.lnp, pop(pair_mask(mate)))
-        both = T.LNI[:, LC * pa:LC * pb + LC]
-        fused([([(cores[d], both) for d in fw], both, sem["ln%d" % (pa // 2)], off)])
-    carry = [(k, hs) for k, hs in relay.items() if core in hs]
-    for (s, d), hs in carry:
-        g.wait_ge(sem.lnp, pop(pair_mask(mate)))
-        relay_ln(s, d, hs)
-
-    g.wait_ge(sem.ldx, 16)
-    mt = slot(mate, r)
-    msem = sem.xl if mate > r else sem.xr
-    nxt = [d for d in (r - 1, r + 1) if 0 <= d < N and d != mate]
-    if mylr:
-        hs = relay[mylr[0]]
-        w = J // len(hs)
-        items = []
-        rest = J
-        for i, h in enumerate(hs):
-            m = part(full, i, len(hs))
-            src = T.W[:, me + w * i:me + w * i + w]
-            if h == cores[mate]:
-                items.append(([(h, T.W[:, mt + w * i:mt + w * i + w])], src, sem.xf, m))
-                rest = w * i
-            else:
-                items.append(([(h, T.HB[:, 0:w])], src, sem.hx, m))
-        fused(items)
-        send(cores[mate], T.W[:, mt:mt + rest], T.W[:, me:me + rest], msem, full)
-    elif nxt:
-        d = nxt[0]
-        od = slot(d, r)
-        fused([([(cores[d], T.W[:, od:od + J])], T.W[:, me:me + J], sem.xl if d > r else sem.xr, off),
-               ([(cores[mate], T.W[:, mt:mt + J])], T.W[:, me:me + J], msem, up)])
+        both = both_lists(r)
+        fused([([(cores[d], both) for d in fw], both, sem["ln%d" % (r // 2)], offmask(core))])
+    if r in half:
+        g.wait_ge(sem.ldy, 16)
+        to_both(r, wx(r, r, H, H), H, H)
+    elif r in own_relay:
+        rest = [0, J]
+        for ph in (0, 1):
+            g.wait_ge(sem.ldy if ph else sem.ldx, 16)
+            items = []
+            for c, o, w, p, m, ln, too in own_relay[r][1]:
+                if p == ph:
+                    if c == cores[mate]:
+                        items.append(([(c, wx(mate, r, o, w))], wx(r, r, o, w), sem.xf, m))
+                        rest[1] = o
+                    else:
+                        items.append(([(c, T.HB[:, 0:w])], wx(r, r, o, w), sem.hx, m))
+                        if too:
+                            rest[0] = o + w
+            fused(items)
+        a, w = rest[0], rest[1] - rest[0]
+        send(cores[mate], wx(mate, r, a, w), wx(r, r, a, w), xsem(mate, r), full)
     else:
-        send(cores[mate], T.W[:, mt:mt + J], T.W[:, me:me + J], msem, up if carry else full)
-    for (s, d), hs in carry:
-        w = J // len(hs)
-        i = hs.index(core)
-        a, o = slot(r, s) + w * i, slot(d, s) + w * i
-        g.wait_ge(sem.xf, pop(topo.mask(cores[s], core)) // len(hs))
-        send(cores[d], T.W[:, o:o + w], T.W[:, a:a + w], sem.xr, topo.mask(core, cores[d]))
+        g.wait_ge(sem.ldx, 16)
+        g.wait_ge(sem.ldy, 16)
+        send(cores[mate], wx(mate, r, 0, J), wx(r, r, 0, J), xsem(mate, r), full)
+    for (s, d), hs in relay.items():
+        for c, o, w, ph, m, ln, too in hs:
+            if c == core:
+                g.wait_ge(sem.xf, pop(m))
+                send(cores[d], wx(d, s, o, w), wx(r, s, o, w), xsem(d, s), offmask(core))
     g.wait_ge(sem.ls, local[0])
 
-    def xcount(s):
-        nm = sem.xl if s < r else sem.xr
-        if (s, r) in relay:
-            return [(nm, sum(pop(topo.mask(h, core)) for h in relay[(s, r)]))]
-        c = cores[s]
-        fm = topo.mask(c, core)
-        if topo.chip(c) != topo.chip(core):
-            return [(nm, pop(fm))]
-        mine = [k for k in relay if k[0] == s]
-        if mine:
-            res = [(nm, pop(fm))]
-            hs = relay[mine[0]]
-            if core in hs:
-                res.append((sem.xf, pop(fm) // len(hs)))
-            return res
-        reach = [q for q in (s - 1, s + 1) if 0 <= q < N and q != r]
-        carries = [1 for hs in relay.values() if c in hs]
-        if reach or carries:
-            return [(nm, pop(fm & ~offmask(c)))]
-        return [(nm, pop(fm))]
-
-    xwaits = [(sem.ldx, 16)]
+    xwaits = [(sem.ldx, 16), (sem.ldy, 16)]
     for s in (r - 1, r + 1):
-        if 0 <= s < N:
-            xwaits += xcount(s)
+        if not 0 <= s < N:
+            continue
+        if s in half:
+            cs = (cores[s], half[s][0])
+            n = sum(pop(upper(c, core) if topo.chip(c) == topo.chip(core) else offmask(c)) for c in cs)
+        elif (s, r) in relay:
+            n = sum(pop(offmask(e[0])) for e in relay[(s, r)])
+        else:
+            n = pop(topo.mask(cores[s], core))
+            for e in own_relay.get(s, (0, []))[1]:
+                if e[0] == core:
+                    xwaits.append((sem.xf, pop(e[4])))
+                elif e[6]:
+                    n += pop(upper(e[0], core))
+        xwaits.append((xsem(r, s), n))
     lwaits = [(sem.ldl, 16), (sem.lnp, pop(pair_mask(mate)))]
     if (r + 1, r) in relay:
-        lwaits.append((sem.lnu, sum(pop(topo.mask(h, core)) for h in relay[(r + 1, r)])))
-    elif r + 1 < N and r + 1 != mate:
-        lwaits = lwaits
-    for p in range(pa // 2):
-        who = [q for q in (2 * p, 2 * p + 1) if r in forwards(q)][0]
-        lwaits.append((sem["ln%d" % p], pop(offmask(cores[who]))))
+        lwaits.append((sem.lnu, sum(pop(offmask(e[0])) for e in relay[(r + 1, r)] if e[5])))
+    for p in range(r // 2):
+        lwaits.append((sem["ln%d" % p], pop(offmask(cores[2 * p]))))
 
     V, SC, PE = g.vector, g.scalar, g.tensor
     nv, nsc, nt = [0], [0], [0]
@@ -287,86 +269,86 @@ def rank_program(g, core, T, topo):
     nb = 8 * ns
     hb = nb // 2
     nc = nl * LC
-    o = 1 + LC * lo
+    o = LC * lo
     zc = ns * J
-    v(V.memset(T.ONE[:, 0:nc + 1], 1.0))
-    v(V.memset(T.F[:, 0:1], 0.0))
-    v(V.memset(T.ZF[:], 0.0))
+    v(V.memset(T.ONE[:, 0:nc], 1.0))
+    v(V.memset(T.CU[:, 0:1], -32.0 * r))
     v(V.memset(T.W[:, zc:zc + 4], 0.0))
-    V.wait_ge(sem.gi, gi[0])
-    v(V.tensor_copy(T.PF[:], T.PI[:]))
+    v(V.memset(T.S[:, 0:hb, R:2 * R], 0.0))
+    v(V.memset(T.S[:, hb:nb, 0:R], 0.0))
+    V.wait_ge(sem.gi, 1)
     v(V.tensor_scalar(T.CI[:], T.PI[:], 7, None, A.bitwise_and))
-    k = v(V.tensor_scalar(T.BI[:], T.PI[:], 63, None, A.bitwise_and))
+    k = v(V.tensor_scalar(T.BI[:], T.PI[:], R - 1, None, A.bitwise_and))
+    v(V.tensor_copy(T.PF[:], T.PI[:]))
     V.wait_ge(sem.v, k)
     v(V.tensor_copy(T.CF[:], T.CI[:]))
-    v(V.tensor_copy(T.PT[:, 0:1], T.ZF[:]))
     k = v(V.tensor_copy(T.BF[:], T.BI[:]))
     V.wait_ge(sem.v, k)
+    V.wait_ge(sem.gi, 3)
     v(V.tensor_scalar(T.XZ[:], T.CCR[:], T.CF[:], None, A.is_equal))
     k = v(V.tensor_scalar(T.XT[:], T.PR[:], T.PF[:], None, A.is_ge))
     v(V.tensor_scalar(T.X2[:], T.CCR[:], T.CF[:], None, A.is_gt))
     v(V.tensor_scalar(T.XY[:], T.CCR[:], T.CF[:], None, A.is_lt))
     V.wait_ge(sem.v, k)
     v(V.tensor_tensor(T.XV[:], T.XZ[:], T.XT[:], A.mult))
-    v(V.tensor_scalar(T.E63[:], T.BF[:], 63.0, None, A.is_equal))
-    v(V.tensor_scalar(T.E64[:], T.BF[:], 63.0, 1.0, A.is_equal, A.subtract))
-    for h in range(4):
+    v(V.tensor_scalar(T.RA[:, 0:AW + 1], T.PR[:, 0:AW + 1], float(R), None, A.mult))
+    v(V.tensor_scalar(T.EL[:], T.BF[:], R - 1.0, None, A.is_equal))
+    v(V.tensor_scalar(T.EM[:], T.BF[:], R - 1.0, 1.0, A.is_equal, A.subtract))
+    for h in range(NH):
         k = v(V.tensor_scalar(T.BH[:, h:h + 1], T.BF[:], 16.0 * h, None, A.subtract))
-    v(V.memset(T.S[:, 0:hb, 64:128], 0.0))
-    v(V.memset(T.S[:, hb:nb, 0:64], 0.0))
+    V.wait_ge(sem.gi, 4)
     V.wait_ge(sem.v, k)
-    for h in range(4):
+    for h in range(NH):
         cs = slice(128 * h, 128 * h + 128)
-        v(V.tensor_scalar(T.CA[:, cs], T.QR[:], T.BH[:, h:h + 1], T.E63[:], A.is_equal, A.add))
-        v(V.tensor_scalar(T.CB[:, cs], T.QR[:], T.BH[:, h:h + 1], T.E64[:], A.not_equal, A.add))
+        v(V.tensor_scalar(T.CA[:, cs], T.QR[:], T.BH[:, h:h + 1], T.EL[:], A.is_equal, A.add))
+        v(V.tensor_scalar(T.CB[:, cs], T.QR[:], T.BH[:, h:h + 1], T.EM[:], A.not_equal, A.add))
 
     for q, n in lwaits:
         V.wait_ge(q, n)
-    vf = v(V.tensor_copy(T.F[:, 1:nc + 1], T.LNI[:, 0:nc]))
-    V.wait_ge(sem.v, vf)
-    vs = v(V.tensor_tensor_scan(T.CU[:, 0:nc + 1], T.ONE[:, 0:nc + 1], T.F[:, 0:nc + 1], -32.0 * r, A.mult, A.add))
-    PE.wait_ge(sem.v, vf)
+    vs = v(V.tensor_tensor_scan(T.CU[:, 1:nc + 1], T.ONE[:, 0:nc], T.LNI[:, 0:nc], -32.0 * r, A.mult, A.add))
+    vf = v(V.tensor_copy(T.F[:, 0:nb], T.LNI[:, o:o + nb]))
     EA, EO = T.psE[:, 0:nb], T.psE[:, 32:32 + ns]
-    t(PE.matmul(EA, T.XV[:], T.F[:, o:o + nb], True, False))
     PE.wait_ge(sem.v, vs)
-    t(PE.matmul(EA, T.XZ[:], T.CU[:, o - 1:o - 1 + nb], False, True))
-    t(PE.matmul(EO, T.XY[:], T.CU[:, o - 1:o - 1 + nb:8], True, False))
-    ke = t(PE.matmul(EO, T.X2[:], T.CU[:, o + 7:o + 7 + 8 * ns - 7:8], False, True))
+    t(PE.matmul(EO, T.XY[:], T.CU[:, o:o + nb:8], True, False))
+    t(PE.matmul(EO, T.X2[:], T.CU[:, o + 8:o + nb + 1:8], False, True))
+    t(PE.matmul(EA, T.XZ[:], T.CU[:, o:o + nb], True, False))
+    PE.wait_ge(sem.v, vf)
+    ke = t(PE.matmul(EA, T.XV[:], T.F[:, 0:nb], False, True))
     V.wait_ge(sem.t, ke)
     for i in range(ns):
-        k = v(V.tensor_scalar(T.EF[:, 8 * i:8 * i + 8], T.psE[:, 8 * i:8 * i + 8], T.psE[:, 32 + i:33 + i], 0.0,
-                              A.add, A.max))
+        k = v(V.tensor_scalar(T.EI[:, 8 * i:8 * i + 8], T.psE[:, 8 * i:8 * i + 8], T.psE[:, 32 + i:33 + i], None,
+                              A.add))
     V.wait_ge(sem.v, k)
-    k = v(V.tensor_copy(T.EI[:, 0:nb], T.EF[:, 0:nb]))
-    V.wait_ge(sem.v, k)
-    k = v(V.tensor_scalar(T.EB[:, 0:nb], T.EI[:, 0:nb], 63, None, A.bitwise_and))
+    k = v(V.tensor_scalar(T.EB[:, 0:nb], T.EI[:, 0:nb], R - 1, None, A.bitwise_and))
+    kf = v(V.tensor_copy(T.EF[:, 0:nb], T.EI[:, 0:nb]))
     V.wait_ge(sem.v, k)
     kb = v(V.tensor_scalar(T.BB[:, 0:nb], T.EB[:, 0:nb], -1.0, 0.5, A.mult, A.add))
 
     ku, ks = [], []
+    V.wait_ge(sem.v, kf)
     for b in range(nb):
-        ku.append(v(V.tensor_scalar(T.U[:, 64 * b:64 * b + 64], T.RA[:], T.EF[:, b:b + 1], None, A.is_gt)))
-    SC.wait_ge(sem.gi, gi[0])
+        ku.append(v(V.tensor_scalar(T.U[:, US * b:US * b + AW + 1], T.RA[:, 0:AW + 1], T.EF[:, b:b + 1], None,
+                                    A.is_gt)))
+    SC.wait_ge(sem.gi, 4)
     SC.wait_ge(sem.v, kb)
     for b in range(nb):
-        c0 = 0 if b < hb else 64
-        ks.append(sc(SC.activation(T.S[:, b, c0:c0 + 64], T.RB[:], ActivationFunctionType.Sign,
+        c0 = 0 if b < hb else R
+        ks.append(sc(SC.activation(T.S[:, b, c0:c0 + R], T.PR[:, 0:R], ActivationFunctionType.Sign,
                                    bias=T.BB[:, b:b + 1], scale=1.0)))
-    for b in range(0, nb, 2):
-        PE.wait_ge(sem.v, ku[b + 1])
-        PE.wait_ge(sem.s, ks[b + 1])
-        for e in (b, b + 1):
-            kp = t(PE.matmul(T.psP[:, 0:64], T.S[:, e, :], T.U[:, 64 * e:64 * e + 64], e == 0, e == nb - 1))
+    for b in range(nb):
+        PE.wait_ge(sem.v, ku[b])
+        PE.wait_ge(sem.s, ks[b])
+        kp = t(PE.matmul(T.psP[:, 0:AW + 1], T.S[:, b, :], T.U[:, US * b:US * b + AW + 1], b == 0, b == nb - 1))
     V.wait_ge(sem.t, kp)
-    k = v(V.tensor_copy(T.PT[:, 1:65], T.psP[:, 0:64]))
+    k = v(V.tensor_copy(T.PT[:, 0:AW + 1], T.psP[:, 0:AW + 1]))
     PE.wait_ge(sem.v, k)
-    for h in range(4):
+    for h in range(NH):
         cs = slice(128 * h, 128 * h + 128)
         po = T["psO%d" % h]
-        t(PE.matmul(po[:, 0:64], T.CA[:, cs], T.PT[:, 1:65], True, False))
-        k = t(PE.matmul(po[:, 0:64], T.CB[:, cs], T.PT[:, 0:64], False, True))
+        t(PE.matmul(po[:, 0:AW], T.CA[:, cs], T.PT[:, 1:AW + 1], True, False))
+        k = t(PE.matmul(po[:, 0:AW], T.CB[:, cs], T.PT[:, 0:AW], False, True))
         V.wait_ge(sem.t, k)
-        vo = v(V.tensor_scalar(T.OFF[:, h:256:4], po[:, 0:64], 0.5, None, A.mult))
+        vo = v(V.tensor_scalar(T.OFF[:, h:256:NH], po[:, 0:AW], 0.5, None, A.mult))
 
     for q, n in xwaits:
         V.wait_ge(q, n)

@@ -4,20 +4,24 @@ from concourse.mybir import AluOpType, ActivationFunctionType
 N, J, Q = 6, 1024, 4096
 H = J // 2
 LC = 8
-CH = [384, 1024, 640]
+CH = [160, 352, 640, 896]
+KV = 5
 R = 64
 AW = Q // R
 NH = R // 16
 US = AW + 2
 
 SCRATCH = {k: ("sbuf", [128, n], "int32") for k, n in
-           {"LNI": 48, "PI": 1, "CI": 1, "BI": 1, "EI": 24, "EB": 24}.items()}
+           {"LNI": 48, "PI": 1, "CI": 1, "BI": 1, "EI": 24, "EB": 24, "PRI": 128, "CCR": 128}.items()}
 SCRATCH.update({k: ("sbuf", [128, n], "float32") for k, n in {
-    "W": 3 * J + 4, "Y": Q, "HB": H, "F": 24, "CU": 49, "ONE": 49, "CCR": 128, "PR": 128, "QR": 128,
-    "PF": 1, "CF": 1, "BF": 1, "EL": 1, "EM": 1, "BH": NH, "X2": 128, "XY": 128, "XZ": 128, "XT": 128,
-    "XV": 128, "EF": 24, "BB": 24}.items()})
+    "W": 3 * J + 4, "Y": Q, "HB": H, "CU": 49, "ONE": 128, "PR": 128,
+    "PF": 1, "CF": 1, "BF": 1, "EL": 1, "EM": 1, "BH": NH, "EF": 24, "BB": 24}.items()})
 SCRATCH.update({
     "RA": ("sbuf", [128, US], "bfloat16"),
+    "NR": ("sbuf", [128, R], "bfloat16"),
+    "QR": ("sbuf", [128, 128], "bfloat16"),
+    "C1": ("sbuf", [128, 50], "float16"),
+    "C2": ("sbuf", [128, 50], "float16"),
     "CA": ("sbuf", [128, 128 * NH], "float16"),
     "CB": ("sbuf", [128, 128 * NH], "float16"),
     "U": ("sbuf", [128, 24 * US], "bfloat16"),
@@ -25,8 +29,10 @@ SCRATCH.update({
     "PT": ("sbuf", [128, US], "float16"),
     "OFF": ("sbuf", [128, 256], "uint16"),
 })
-SCRATCH.update({k: ("psum", [128, 512], "float32") for k in ["psE", "psP"] + ["psO%d" % h for h in range(NH)]})
-SEMAPHORES = ["ldl", "ldx", "ldy", "lnp", "lnu", "ln0", "ln1", "xl", "xr", "xf", "hx", "ls", "gi", "v", "s", "t", "ys"]
+SCRATCH.update({k: ("sbuf", [128, 128], "float16") for k in ("X2", "XY", "XZ", "XT", "XV", "XW")})
+SCRATCH.update({k: ("psum", [128, 512], "float32") for k in ["psE", "psF", "psP"] + ["psO%d" % h for h in range(NH)]})
+SEMAPHORES = ["ldl", "ldx", "ldy", "lnp", "lnu", "ln0", "ln1", "xl", "xr", "xf", "hx", "ls", "gi", "v", "s", "t", "ys",
+              "cr", "cq"]
 
 
 def bits(m):
@@ -80,6 +86,22 @@ def plan(cores, topo):
     return half, relay
 
 
+def makers(cores, topo):
+    half, relay = plan(cores, topo)
+    cs = {c for c, _ in half.values()} | {e[0] for hs in relay.values() for e in hs}
+    by_chip = {}
+    for c in sorted(cs - set(cores)):
+        by_chip.setdefault(topo.chip(c), []).append(c)
+    res = {}
+    for ch, l in by_chip.items():
+        o, res[ch] = 0, []
+        for i, c in enumerate(l):
+            k = -(-(8 - o) // (len(l) - i))
+            res[ch].append((c, 16 * o, 16 * k))
+            o += k
+    return res
+
+
 def rank_program(g, core, T, topo):
     A = AluOpType
     sem = T.sem
@@ -119,7 +141,7 @@ def rank_program(g, core, T, topo):
         return T.W[:, slot(d, s) + a:slot(d, s) + a + w]
 
     def pair_mask(q):
-        return topo.mask(cores[q], cores[q ^ 1]) if q in own_relay else upper(cores[q], cores[q ^ 1])
+        return topo.mask(cores[q], cores[q ^ 1])
 
     def forwards(q):
         a, b = min(q, q ^ 1), max(q, q ^ 1)
@@ -135,13 +157,20 @@ def rank_program(g, core, T, topo):
                ([(cores[m], wx(m, s, a, w))], src, xsem(m, s), upper(core, cores[m]))])
 
     if rank is None:
+        for c, a, w in makers(cores, topo).get(topo.chip(core), []):
+            if c == core:
+                qr = T.QR[:, a:a + w]
+                g.iota(qr, [[0, w // 16], [1, 16]], 0, 0, allow_small_or_imprecise_dtypes=True).then_inc(sem.gi, 1)
+                g.wait_ge(sem.gi, 1)
+                ds = [q for q in cores if topo.chip(q) == topo.chip(core)]
+                fused([([(q, qr) for q in ds], qr, sem.cq, topo.mask(core, ds[0]))])
         for s, (c, d) in half.items():
             if c == core:
                 g.wait_ge(sem.lnp, pop(pair_mask(s)) + pop(pair_mask(s ^ 1)))
                 fw = forwards(s)[1:]
                 both = both_lists(s)
                 fused([([(cores[q], both) for q in fw], both, sem["ln%d" % (s // 2)], offmask(core))])
-                g.wait_ge(sem.hx, pop(topo.mask(cores[s], core)))
+                g.wait_ge(sem.hx, pop(upper(cores[s], core)))
                 to_both(s, T.HB[:], 0, H)
                 g.wait_ge(sem.ls, local[0])
         for (s, d), hs in relay.items():
@@ -176,25 +205,25 @@ def rank_program(g, core, T, topo):
     g.sync.dma_start(T.W[:, me + H:me + J], T.x[:, H:J]).then_inc(sem.ldy, 16)
 
     g.iota(T.PI[:], [[0, 1]], 0, 1).then_inc(sem.gi, 1)
-    for buf, pat in ((T.CCR, [[0, 16], [1, 8]]), (T.PR, [[1, 128]]), (T.QR, [[0, 8], [1, 16]])):
-        g.iota(buf[:], pat, 0, 0, allow_small_or_imprecise_dtypes=True).then_inc(sem.gi, 1)
+    row, pat = (T.RA[:, 0:AW + 1], [[R, AW + 1]]) if r < mate else (T.NR[:], [[-1, R]])
+    g.iota(row, pat, 0, 0, allow_small_or_imprecise_dtypes=True).then_inc(sem.gi, 1)
+    g.wait_ge(sem.gi, 2)
+    send(cores[mate], row, row, sem.cr, pair_mask(r))
 
     g.wait_ge(sem.ldl, 16)
-    dsts = []
+    dsts = [cores[mate]]
     if r in own_relay:
         dsts += [e[0] for e in own_relay[r][1] if e[5]]
     dsts += [half[q][0] for q in (r, mate) if q in half]
-    dsts.append(cores[mate])
     fused([([(c, own) for c in dsts], own, sem.lnp, pair_mask(r))])
-    if r in half:
-        g.wait_ge(sem.ldx, 16)
-        send(half[r][0], T.HB[:], wx(r, r, 0, H), sem.hx, topo.mask(core, half[r][0]))
     fw = forwards(r)[:1] if r in half else forwards(r)
     if fw:
         g.wait_ge(sem.lnp, pop(pair_mask(mate)))
         both = both_lists(r)
         fused([([(cores[d], both) for d in fw], both, sem["ln%d" % (r // 2)], offmask(core))])
     if r in half:
+        g.wait_ge(sem.ldx, 16)
+        send(half[r][0], T.HB[:], wx(r, r, 0, H), sem.hx, upper(core, half[r][0]))
         g.wait_ge(sem.ldy, 16)
         to_both(r, wx(r, r, H, H), H, H)
     elif r in own_relay:
@@ -271,11 +300,18 @@ def rank_program(g, core, T, topo):
     nc = nl * LC
     o = LC * lo
     zc = ns * J
-    v(V.memset(T.ONE[:, 0:nc], 1.0))
-    v(V.memset(T.CU[:, 0:1], -32.0 * r))
+    k = v(V.memset(T.ONE[:], 1.0))
+    V.wait_ge(sem.v, k)
+    v(V.tensor_tensor_scan(T.PR[:], T.ONE[:], T.ONE[:], -1.0, A.mult, A.add))
+    k = v(V.memset(T.CU[:, 0:1], -32.0 * r))
     v(V.memset(T.W[:, zc:zc + 4], 0.0))
     v(V.memset(T.S[:, 0:hb, R:2 * R], 0.0))
     v(V.memset(T.S[:, hb:nb, 0:R], 0.0))
+    V.wait_ge(sem.v, k)
+    k = v(V.tensor_copy(T.PRI[:], T.PR[:]))
+    v(V.tensor_copy(T.C1[:, 0:1], T.CU[:, 0:1]))
+    V.wait_ge(sem.v, k)
+    v(V.tensor_scalar(T.CCR[:], T.PRI[:], 7, None, A.bitwise_and))
     V.wait_ge(sem.gi, 1)
     v(V.tensor_scalar(T.CI[:], T.PI[:], 7, None, A.bitwise_and))
     k = v(V.tensor_scalar(T.BI[:], T.PI[:], R - 1, None, A.bitwise_and))
@@ -284,20 +320,22 @@ def rank_program(g, core, T, topo):
     v(V.tensor_copy(T.CF[:], T.CI[:]))
     k = v(V.tensor_copy(T.BF[:], T.BI[:]))
     V.wait_ge(sem.v, k)
-    V.wait_ge(sem.gi, 3)
+    v(V.tensor_scalar(T.EL[:], T.BF[:], R - 1.0, None, A.is_equal))
+    v(V.tensor_scalar(T.EM[:], T.BF[:], R - 1.0, 1.0, A.is_equal, A.subtract))
+    for h in range(NH):
+        k = v(V.tensor_scalar(T.BH[:, h:h + 1], T.BF[:], 16.0 * h, None, A.subtract))
+    V.wait_ge(sem.v, k)
     v(V.tensor_scalar(T.XZ[:], T.CCR[:], T.CF[:], None, A.is_equal))
     k = v(V.tensor_scalar(T.XT[:], T.PR[:], T.PF[:], None, A.is_ge))
     v(V.tensor_scalar(T.X2[:], T.CCR[:], T.CF[:], None, A.is_gt))
     v(V.tensor_scalar(T.XY[:], T.CCR[:], T.CF[:], None, A.is_lt))
     V.wait_ge(sem.v, k)
-    v(V.tensor_tensor(T.XV[:], T.XZ[:], T.XT[:], A.mult))
-    v(V.tensor_scalar(T.RA[:, 0:AW + 1], T.PR[:, 0:AW + 1], float(R), None, A.mult))
-    v(V.tensor_scalar(T.EL[:], T.BF[:], R - 1.0, None, A.is_equal))
-    v(V.tensor_scalar(T.EM[:], T.BF[:], R - 1.0, 1.0, A.is_equal, A.subtract))
-    for h in range(NH):
-        k = v(V.tensor_scalar(T.BH[:, h:h + 1], T.BF[:], 16.0 * h, None, A.subtract))
-    V.wait_ge(sem.gi, 4)
+    k = v(V.tensor_tensor(T.XV[:], T.XZ[:], T.XT[:], A.mult))
     V.wait_ge(sem.v, k)
+    v(V.tensor_tensor(T.XW[:], T.XZ[:], T.XV[:], A.subtract))
+    V.wait_ge(sem.gi, 2)
+    V.wait_ge(sem.cr, pop(pair_mask(mate)))
+    V.wait_ge(sem.cq, sum(pop(topo.mask(e[0], core)) for e in makers(cores, topo)[topo.chip(core)]))
     for h in range(NH):
         cs = slice(128 * h, 128 * h + 128)
         v(V.tensor_scalar(T.CA[:, cs], T.QR[:], T.BH[:, h:h + 1], T.EL[:], A.is_equal, A.add))
@@ -305,40 +343,56 @@ def rank_program(g, core, T, topo):
 
     for q, n in lwaits:
         V.wait_ge(q, n)
-    vs = v(V.tensor_tensor_scan(T.CU[:, 1:nc + 1], T.ONE[:, 0:nc], T.LNI[:, 0:nc], -32.0 * r, A.mult, A.add))
-    vf = v(V.tensor_copy(T.F[:, 0:nb], T.LNI[:, o:o + nb]))
-    EA, EO = T.psE[:, 0:nb], T.psE[:, 32:32 + ns]
-    PE.wait_ge(sem.v, vs)
-    t(PE.matmul(EO, T.XY[:], T.CU[:, o:o + nb:8], True, False))
-    t(PE.matmul(EO, T.X2[:], T.CU[:, o + 8:o + nb + 1:8], False, True))
-    t(PE.matmul(EA, T.XZ[:], T.CU[:, o:o + nb], True, False))
-    PE.wait_ge(sem.v, vf)
-    ke = t(PE.matmul(EA, T.XV[:], T.F[:, 0:nb], False, True))
+
+    def scan(out):
+        return v(V.tensor_tensor_scan(out[:, 1:nc + 1], T.ONE[:, 0:nc], T.LNI[:, 0:nc], -32.0 * r, A.mult, A.add))
+
+    v1 = scan(T.C1)
+    vf = scan(T.CU)
+    V.wait_ge(sem.v, vf)
+    v2 = v(V.tensor_tensor(T.C2[:, 0:nc + 1], T.CU[:, 0:nc + 1], T.C1[:, 0:nc + 1], A.subtract))
+    EA, EO = T.psE[:, 0:nb], T.psF[:, 0:ns]
+    for i, (kc, C) in enumerate(((v1, T.C1), (v2, T.C2))):
+        PE.wait_ge(sem.v, kc)
+        t(PE.matmul(EO, T.XY[:], C[:, o:o + nb:8], i == 0, False))
+        t(PE.matmul(EO, T.X2[:], C[:, o + 8:o + nb + 1:8], False, i == 1))
+        t(PE.matmul(EA, T.XV[:], C[:, o + 1:o + nb + 1], i == 0, False))
+        ke = t(PE.matmul(EA, T.XW[:], C[:, o:o + nb], False, i == 1))
     V.wait_ge(sem.t, ke)
     for i in range(ns):
-        k = v(V.tensor_scalar(T.EI[:, 8 * i:8 * i + 8], T.psE[:, 8 * i:8 * i + 8], T.psE[:, 32 + i:33 + i], None,
-                              A.add))
+        k = v(V.tensor_scalar(T.EI[:, 8 * i:8 * i + 8], T.psE[:, 8 * i:8 * i + 8], T.psF[:, i:i + 1], None, A.add))
     V.wait_ge(sem.v, k)
     k = v(V.tensor_scalar(T.EB[:, 0:nb], T.EI[:, 0:nb], R - 1, None, A.bitwise_and))
     kf = v(V.tensor_copy(T.EF[:, 0:nb], T.EI[:, 0:nb]))
     V.wait_ge(sem.v, k)
     kb = v(V.tensor_scalar(T.BB[:, 0:nb], T.EB[:, 0:nb], -1.0, 0.5, A.mult, A.add))
 
-    ku, ks = [], []
-    V.wait_ge(sem.v, kf)
-    for b in range(nb):
-        ku.append(v(V.tensor_scalar(T.U[:, US * b:US * b + AW + 1], T.RA[:, 0:AW + 1], T.EF[:, b:b + 1], None,
-                                    A.is_gt)))
-    SC.wait_ge(sem.gi, 4)
     SC.wait_ge(sem.v, kb)
-    for b in range(nb):
+    V.wait_ge(sem.v, kf)
+    ready = {}
+    order = list(range(nb - KV))
+    for i in range(KV):
+        order.insert(4 * i + 3 if nb > 16 else 3 * i + 2, nb - KV + i)
+    waited = False
+    for b in order:
         c0 = 0 if b < hb else R
-        ks.append(sc(SC.activation(T.S[:, b, c0:c0 + R], T.PR[:, 0:R], ActivationFunctionType.Sign,
-                                   bias=T.BB[:, b:b + 1], scale=1.0)))
-    for b in range(nb):
-        PE.wait_ge(sem.v, ku[b])
-        PE.wait_ge(sem.s, ks[b])
-        kp = t(PE.matmul(T.psP[:, 0:AW + 1], T.S[:, b, :], T.U[:, US * b:US * b + AW + 1], b == 0, b == nb - 1))
+        us, sb = T.U[:, US * b:US * b + AW + 1], T.S[:, b, c0:c0 + R]
+        if b < nb - KV:
+            ku = v(V.tensor_scalar(us, T.RA[:, 0:AW + 1], T.EF[:, b:b + 1], None, A.is_gt))
+            ks = (sem.s, sc(SC.activation(sb, T.PR[:, 0:R], ActivationFunctionType.Sign, bias=T.BB[:, b:b + 1],
+                                          scale=1.0)))
+        else:
+            if not waited:
+                V.wait_ge(sem.v, kb)
+                waited = True
+            ku = v(V.tensor_scalar(us, T.RA[:, 0:AW + 1], T.EF[:, b:b + 1], 2.0, A.is_gt, A.mult))
+            ks = (sem.v, v(V.tensor_scalar(sb, T.NR[:], T.BB[:, b:b + 1], 0.5, A.is_lt, A.subtract)))
+        ready[b] = [(sem.v, ku), ks]
+    for b in order:
+        for q, n in ready[b]:
+            PE.wait_ge(q, n)
+        kp = t(PE.matmul(T.psP[:, 0:AW + 1], T.S[:, b, :], T.U[:, US * b:US * b + AW + 1], b == order[0],
+                         b == order[-1]))
     V.wait_ge(sem.t, kp)
     k = v(V.tensor_copy(T.PT[:, 0:AW + 1], T.psP[:, 0:AW + 1]))
     PE.wait_ge(sem.v, k)
@@ -357,15 +411,16 @@ def rank_program(g, core, T, topo):
     SC.wait_ge(sem.v, vo)
     win = T.W[:, 0:zc + 4]
     c = 0
-    order = []
+    pieces = []
     for w in CH:
-        d = c + Q // 2
-        kv = v(V.tensor_copy(T.Y[:, c:c + w], win.indirect(T.OFF[:, c // 16:(c + w) // 16])))
+        d = c + w
+        kv = v(V.tensor_copy(T.Y[:, c:d], win.indirect(T.OFF[:, c // 16:d // 16])))
         k2 = sc(SC.activation(T.Y[:, d:d + w], win.indirect(T.OFF[:, d // 16:(d + w) // 16]),
                               ActivationFunctionType.Copy))
-        order += [(sem.v, kv, c, w), (sem.s, k2, d, w)]
-        c += w
-    for q, n, c, w in order:
-        g.sync.wait_ge(q, n)
+        pieces.append((kv, k2, c, 2 * w))
+        c += 2 * w
+    for kv, k2, c, w in pieces:
+        g.sync.wait_ge(sem.v, kv)
+        g.sync.wait_ge(sem.s, k2)
         g.sync.dma_start(T.y[:, c:c + w], T.Y[:, c:c + w]).then_inc(sem.ys, 16)
-    g.sync.wait_ge(sem.ys, 16 * len(order))
+    g.sync.wait_ge(sem.ys, 16 * len(pieces))

from concourse.bass import DstId, RemoteDMATransfer
from concourse.mybir import AluOpType, ActivationFunctionType

N, J, Q = 6, 1024, 4096
H = J // 2
LC = 8
CH = [160, 352, 640, 896]
KV = 5
R = 64
AW = Q // R
NH = R // 16
US = AW + 2

SCRATCH = {k: ("sbuf", [128, n], "int32") for k, n in
           {"LNI": 48, "PI": 1, "CI": 1, "BI": 1, "EI": 24, "EB": 24, "PRI": 128, "CCR": 128}.items()}
SCRATCH.update({k: ("sbuf", [128, n], "float32") for k, n in {
    "W": 3 * J + 4, "Y": Q, "HB": H, "CU": 49, "ONE": 128, "PR": 128,
    "PF": 1, "CF": 1, "BF": 1, "EL": 1, "EM": 1, "BH": NH, "EF": 24, "BB": 24}.items()})
SCRATCH.update({
    "RA": ("sbuf", [128, US], "bfloat16"),
    "NR": ("sbuf", [128, R], "bfloat16"),
    "QR": ("sbuf", [128, 128], "bfloat16"),
    "C1": ("sbuf", [128, 50], "float16"),
    "C2": ("sbuf", [128, 50], "float16"),
    "CA": ("sbuf", [128, 128 * NH], "float16"),
    "CB": ("sbuf", [128, 128 * NH], "float16"),
    "U": ("sbuf", [128, 24 * US], "bfloat16"),
    "S": ("sbuf", [128, 24, 2 * R], "bfloat16"),
    "PT": ("sbuf", [128, US], "float16"),
    "OFF": ("sbuf", [128, 256], "uint16"),
})
SCRATCH.update({k: ("sbuf", [128, 128], "float16") for k in ("X2", "XY", "XZ", "XT", "XV", "XW")})
SCRATCH.update({k: ("psum", [128, 512], "float32") for k in ["psE", "psF", "psP"] + ["psO%d" % h for h in range(NH)]})
SEMAPHORES = ["ldl", "ldx", "ldy", "lnp", "lnu", "ln0", "ln1", "xl", "xr", "xf", "hx", "ls", "gi", "v", "s", "t", "ys",
              "cr", "cq"]


def bits(m):
    return [i for i in range(m.bit_length()) if m >> i & 1]


def pop(m):
    return len(bits(m))


def part(m, i, k):
    b = bits(m)
    n = len(b) // k
    return sum(1 << e for e in b[i * n:(i + 1) * n])


def slot(r, s):
    return J * (s - max(r - 1, 0))


def plan(cores, topo):
    ncores = max(cores) + topo.CORES_PER_CHIP
    pairs = [(s, d) for s in range(N) for d in (s - 1, s + 1)
             if 0 <= d < N and topo.chip(cores[s]) != topo.chip(cores[d])]
    half, relay, used = {}, {}, set()

    def ports(s, d):
        return [c for c in range(ncores) if topo.chip(c) == topo.chip(cores[s]) and c != cores[s]
                and topo.may_write(c, cores[d]) and c not in used]

    for s, d in pairs:
        if topo.may_write(cores[s], cores[d]):
            c = [c for c in ports(s, d) if c not in cores and topo.die(c) != topo.die(cores[s])][-1]
            half[s] = (c, d)
            used.update((c, cores[s]))
    for s, d in pairs:
        if not topo.may_write(cores[s], cores[d]):
            hs = ports(s, d)
            near = [c for c in hs if topo.die(c) == topo.die(cores[s])]
            far = [c for c in hs if topo.die(c) != topo.die(cores[s])]
            phases = [far, near] if len(hs) == 2 else [near, far]
            res, o = [], 0
            for ph, cs in enumerate(phases):
                for i, c in enumerate(cs):
                    w = H // len(cs)
                    ln = (LC // 2 * ph, LC // 2 * ph + LC // 2) if i == 0 else None
                    too = len(cs) == 1 and c not in cores and topo.die(c) == topo.die(cores[s ^ 1])
                    res.append((c, o, w, ph, part(topo.mask(cores[s], c), i, len(cs)), ln, too))
                    o += w
            relay[(s, d)] = res
    return half, relay


def makers(cores, topo):
    half, relay = plan(cores, topo)
    cs = {c for c, _ in half.values()} | {e[0] for hs in relay.values() for e in hs}
    by_chip = {}
    for c in sorted(cs - set(cores)):
        by_chip.setdefault(topo.chip(c), []).append(c)
    res = {}
    for ch, l in by_chip.items():
        o, res[ch] = 0, []
        for i, c in enumerate(l):
            k = -(-(8 - o) // (len(l) - i))
            res[ch].append((c, 16 * o, 16 * k))
            o += k
    return res


def rank_program(g, core, T, topo):
    A = AluOpType
    sem = T.sem
    cores = list(T.cores)
    rank = T.rank_of(core)
    local = [0]
    half, relay = plan(cores, topo)
    own_relay = {k[0]: (k[1], hs) for k, hs in relay.items()}

    def offmask(c):
        return min([topo.mask(c, q) for q in cores if topo.chip(q) != topo.chip(c)])

    def upper(c, d):
        return topo.mask(c, d) & ~offmask(c)

    def send(dst, out, in_, rsem, mask):
        rid, pid, _ = topo.addr(dst)
        g.remote_dma(out, in_, rsem, sem.ls, pid, rid, mask)
        local[0] += pop(mask)

    def fused(items):
        tr = []
        for dsts, in_, rsem, mask in items:
            ids = []
            for d, _ in dsts:
                a = topo.addr(d)
                ids.append(DstId(rid=a[0], pnc=a[1]))
            tr.append(RemoteDMATransfer(dst_ids=ids, dma_engine_mask=mask, remote_sem=rsem, srcs=[in_],
                                        dsts=[o for _, o in dsts]))
            local[0] += pop(mask)
        g.remote_dma_fused(tr, local_sem=sem.ls)

    def xsem(d, s):
        return sem.xl if s < d else sem.xr

    def wx(d, s, a, w):
        return T.W[:, slot(d, s) + a:slot(d, s) + a + w]

    def pair_mask(q):
        return topo.mask(cores[q], cores[q ^ 1])

    def forwards(q):
        a, b = min(q, q ^ 1), max(q, q ^ 1)
        return [d for d in range(b + 1, N) if (a if topo.may_write(cores[a], cores[d]) else b) == q]

    def both_lists(q):
        a = LC * min(q, q ^ 1)
        return T.LNI[:, a:a + 2 * LC]

    def to_both(s, src, a, w):
        d, m = half[s][1], s ^ 1
        fused([([(cores[d], wx(d, s, a, w))], src, xsem(d, s), offmask(core)),
               ([(cores[m], wx(m, s, a, w))], src, xsem(m, s), upper(core, cores[m]))])

    if rank is None:
        for c, a, w in makers(cores, topo).get(topo.chip(core), []):
            if c == core:
                qr = T.QR[:, a:a + w]
                g.iota(qr, [[0, w // 16], [1, 16]], 0, 0, allow_small_or_imprecise_dtypes=True).then_inc(sem.gi, 1)
                g.wait_ge(sem.gi, 1)
                ds = [q for q in cores if topo.chip(q) == topo.chip(core)]
                fused([([(q, qr) for q in ds], qr, sem.cq, topo.mask(core, ds[0]))])
        for s, (c, d) in half.items():
            if c == core:
                g.wait_ge(sem.lnp, pop(pair_mask(s)) + pop(pair_mask(s ^ 1)))
                fw = forwards(s)[1:]
                both = both_lists(s)
                fused([([(cores[q], both) for q in fw], both, sem["ln%d" % (s // 2)], offmask(core))])
                g.wait_ge(sem.hx, pop(upper(cores[s], core)))
                to_both(s, T.HB[:], 0, H)
                g.wait_ge(sem.ls, local[0])
        for (s, d), hs in relay.items():
            for c, o, w, ph, m, ln, too in hs:
                if c == core:
                    if ln:
                        a = T.LNI[:, LC * s + ln[0]:LC * s + ln[1]]
                        g.wait_ge(sem.lnp, pop(pair_mask(s)))
                        send(cores[d], a, a, sem.lnu, offmask(core))
                    g.wait_ge(sem.hx, pop(m))
                    src = T.HB[:, 0:w]
                    if too:
                        q = s ^ 1
                        fused([([(cores[d], wx(d, s, o, w))], src, xsem(d, s), offmask(core)),
                               ([(cores[q], wx(q, s, o, w))], src, xsem(q, s), upper(core, cores[q]))])
                    else:
                        send(cores[d], wx(d, s, o, w), src, xsem(d, s), offmask(core))
                    g.wait_ge(sem.ls, local[0])
        return

    r = rank
    mate = r ^ 1
    me = slot(r, r)
    lo = max(r - 1, 0)
    ns = min(r + 1, N - 1) - lo + 1
    nl = min(r + 2, N)
    full = topo.mask(core, cores[mate])

    own = T.LNI[:, LC * r:LC * r + LC]
    g.sync.dma_start(own, T.ln[:]).then_inc(sem.ldl, 16)
    g.sync.dma_start(T.W[:, me:me + H], T.x[:, 0:H]).then_inc(sem.ldx, 16)
    g.sync.dma_start(T.W[:, me + H:me + J], T.x[:, H:J]).then_inc(sem.ldy, 16)

    g.iota(T.PI[:], [[0, 1]], 0, 1).then_inc(sem.gi, 1)
    row, pat = (T.RA[:, 0:AW + 1], [[R, AW + 1]]) if r < mate else (T.NR[:], [[-1, R]])
    g.iota(row, pat, 0, 0, allow_small_or_imprecise_dtypes=True).then_inc(sem.gi, 1)
    g.wait_ge(sem.gi, 2)
    send(cores[mate], row, row, sem.cr, pair_mask(r))

    g.wait_ge(sem.ldl, 16)
    dsts = [cores[mate]]
    if r in own_relay:
        dsts += [e[0] for e in own_relay[r][1] if e[5]]
    dsts += [half[q][0] for q in (r, mate) if q in half]
    fused([([(c, own) for c in dsts], own, sem.lnp, pair_mask(r))])
    fw = forwards(r)[:1] if r in half else forwards(r)
    if fw:
        g.wait_ge(sem.lnp, pop(pair_mask(mate)))
        both = both_lists(r)
        fused([([(cores[d], both) for d in fw], both, sem["ln%d" % (r // 2)], offmask(core))])
    if r in half:
        g.wait_ge(sem.ldx, 16)
        send(half[r][0], T.HB[:], wx(r, r, 0, H), sem.hx, upper(core, half[r][0]))
        g.wait_ge(sem.ldy, 16)
        to_both(r, wx(r, r, H, H), H, H)
    elif r in own_relay:
        rest = [0, J]
        for ph in (0, 1):
            g.wait_ge(sem.ldy if ph else sem.ldx, 16)
            items = []
            for c, o, w, p, m, ln, too in own_relay[r][1]:
                if p == ph:
                    if c == cores[mate]:
                        items.append(([(c, wx(mate, r, o, w))], wx(r, r, o, w), sem.xf, m))
                        rest[1] = o
                    else:
                        items.append(([(c, T.HB[:, 0:w])], wx(r, r, o, w), sem.hx, m))
                        if too:
                            rest[0] = o + w
            fused(items)
        a, w = rest[0], rest[1] - rest[0]
        send(cores[mate], wx(mate, r, a, w), wx(r, r, a, w), xsem(mate, r), full)
    else:
        g.wait_ge(sem.ldx, 16)
        g.wait_ge(sem.ldy, 16)
        send(cores[mate], wx(mate, r, 0, J), wx(r, r, 0, J), xsem(mate, r), full)
    for (s, d), hs in relay.items():
        for c, o, w, ph, m, ln, too in hs:
            if c == core:
                g.wait_ge(sem.xf, pop(m))
                send(cores[d], wx(d, s, o, w), wx(r, s, o, w), xsem(d, s), offmask(core))
    g.wait_ge(sem.ls, local[0])

    xwaits = [(sem.ldx, 16), (sem.ldy, 16)]
    for s in (r - 1, r + 1):
        if not 0 <= s < N:
            continue
        if s in half:
            cs = (cores[s], half[s][0])
            n = sum(pop(upper(c, core) if topo.chip(c) == topo.chip(core) else offmask(c)) for c in cs)
        elif (s, r) in relay:
            n = sum(pop(offmask(e[0])) for e in relay[(s, r)])
        else:
            n = pop(topo.mask(cores[s], core))
            for e in own_relay.get(s, (0, []))[1]:
                if e[0] == core:
                    xwaits.append((sem.xf, pop(e[4])))
                elif e[6]:
                    n += pop(upper(e[0], core))
        xwaits.append((xsem(r, s), n))
    lwaits = [(sem.ldl, 16), (sem.lnp, pop(pair_mask(mate)))]
    if (r + 1, r) in relay:
        lwaits.append((sem.lnu, sum(pop(offmask(e[0])) for e in relay[(r + 1, r)] if e[5])))
    for p in range(r // 2):
        lwaits.append((sem["ln%d" % p], pop(offmask(cores[2 * p]))))

    V, SC, PE = g.vector, g.scalar, g.tensor
    nv, nsc, nt = [0], [0], [0]

    def v(ins):
        ins.then_inc(sem.v, 1)
        nv[0] += 1
        return nv[0]

    def sc(ins):
        ins.then_inc(sem.s, 1)
        nsc[0] += 1
        return nsc[0]

    def t(ins):
        ins.then_inc(sem.t, 1)
        nt[0] += 1
        return nt[0]

    nb = 8 * ns
    hb = nb // 2
    nc = nl * LC
    o = LC * lo
    zc = ns * J
    k = v(V.memset(T.ONE[:], 1.0))
    V.wait_ge(sem.v, k)
    v(V.tensor_tensor_scan(T.PR[:], T.ONE[:], T.ONE[:], -1.0, A.mult, A.add))
    k = v(V.memset(T.CU[:, 0:1], -32.0 * r))
    v(V.memset(T.W[:, zc:zc + 4], 0.0))
    v(V.memset(T.S[:, 0:hb, R:2 * R], 0.0))
    v(V.memset(T.S[:, hb:nb, 0:R], 0.0))
    V.wait_ge(sem.v, k)
    k = v(V.tensor_copy(T.PRI[:], T.PR[:]))
    v(V.tensor_copy(T.C1[:, 0:1], T.CU[:, 0:1]))
    V.wait_ge(sem.v, k)
    v(V.tensor_scalar(T.CCR[:], T.PRI[:], 7, None, A.bitwise_and))
    V.wait_ge(sem.gi, 1)
    v(V.tensor_scalar(T.CI[:], T.PI[:], 7, None, A.bitwise_and))
    k = v(V.tensor_scalar(T.BI[:], T.PI[:], R - 1, None, A.bitwise_and))
    v(V.tensor_copy(T.PF[:], T.PI[:]))
    V.wait_ge(sem.v, k)
    v(V.tensor_copy(T.CF[:], T.CI[:]))
    k = v(V.tensor_copy(T.BF[:], T.BI[:]))
    V.wait_ge(sem.v, k)
    v(V.tensor_scalar(T.EL[:], T.BF[:], R - 1.0, None, A.is_equal))
    v(V.tensor_scalar(T.EM[:], T.BF[:], R - 1.0, 1.0, A.is_equal, A.subtract))
    for h in range(NH):
        k = v(V.tensor_scalar(T.BH[:, h:h + 1], T.BF[:], 16.0 * h, None, A.subtract))
    V.wait_ge(sem.v, k)
    v(V.tensor_scalar(T.XZ[:], T.CCR[:], T.CF[:], None, A.is_equal))
    k = v(V.tensor_scalar(T.XT[:], T.PR[:], T.PF[:], None, A.is_ge))
    v(V.tensor_scalar(T.X2[:], T.CCR[:], T.CF[:], None, A.is_gt))
    v(V.tensor_scalar(T.XY[:], T.CCR[:], T.CF[:], None, A.is_lt))
    V.wait_ge(sem.v, k)
    k = v(V.tensor_tensor(T.XV[:], T.XZ[:], T.XT[:], A.mult))
    V.wait_ge(sem.v, k)
    v(V.tensor_tensor(T.XW[:], T.XZ[:], T.XV[:], A.subtract))
    V.wait_ge(sem.gi, 2)
    V.wait_ge(sem.cr, pop(pair_mask(mate)))
    V.wait_ge(sem.cq, sum(pop(topo.mask(e[0], core)) for e in makers(cores, topo)[topo.chip(core)]))
    for h in range(NH):
        cs = slice(128 * h, 128 * h + 128)
        v(V.tensor_scalar(T.CA[:, cs], T.QR[:], T.BH[:, h:h + 1], T.EL[:], A.is_equal, A.add))
        v(V.tensor_scalar(T.CB[:, cs], T.QR[:], T.BH[:, h:h + 1], T.EM[:], A.not_equal, A.add))

    for q, n in lwaits:
        V.wait_ge(q, n)

    def scan(out):
        return v(V.tensor_tensor_scan(out[:, 1:nc + 1], T.ONE[:, 0:nc], T.LNI[:, 0:nc], -32.0 * r, A.mult, A.add))

    v1 = scan(T.C1)
    vf = scan(T.CU)
    V.wait_ge(sem.v, vf)
    v2 = v(V.tensor_tensor(T.C2[:, 0:nc + 1], T.CU[:, 0:nc + 1], T.C1[:, 0:nc + 1], A.subtract))
    EA, EO = T.psE[:, 0:nb], T.psF[:, 0:ns]
    for i, (kc, C) in enumerate(((v1, T.C1), (v2, T.C2))):
        PE.wait_ge(sem.v, kc)
        t(PE.matmul(EO, T.XY[:], C[:, o:o + nb:8], i == 0, False))
        t(PE.matmul(EO, T.X2[:], C[:, o + 8:o + nb + 1:8], False, i == 1))
        t(PE.matmul(EA, T.XV[:], C[:, o + 1:o + nb + 1], i == 0, False))
        ke = t(PE.matmul(EA, T.XW[:], C[:, o:o + nb], False, i == 1))
    V.wait_ge(sem.t, ke)
    for i in range(ns):
        k = v(V.tensor_scalar(T.EI[:, 8 * i:8 * i + 8], T.psE[:, 8 * i:8 * i + 8], T.psF[:, i:i + 1], None, A.add))
    V.wait_ge(sem.v, k)
    k = v(V.tensor_scalar(T.EB[:, 0:nb], T.EI[:, 0:nb], R - 1, None, A.bitwise_and))
    kf = v(V.tensor_copy(T.EF[:, 0:nb], T.EI[:, 0:nb]))
    V.wait_ge(sem.v, k)
    kb = v(V.tensor_scalar(T.BB[:, 0:nb], T.EB[:, 0:nb], -1.0, 0.5, A.mult, A.add))

    SC.wait_ge(sem.v, kb)
    V.wait_ge(sem.v, kf)
    ready = {}
    order = list(range(nb - KV))
    for i in range(KV):
        order.insert(4 * i + 3 if nb > 16 else 3 * i + 2, nb - KV + i)
    waited = False
    for b in order:
        c0 = 0 if b < hb else R
        us, sb = T.U[:, US * b:US * b + AW + 1], T.S[:, b, c0:c0 + R]
        if b < nb - KV:
            ku = v(V.tensor_scalar(us, T.RA[:, 0:AW + 1], T.EF[:, b:b + 1], None, A.is_gt))
            ks = (sem.s, sc(SC.activation(sb, T.PR[:, 0:R], ActivationFunctionType.Sign, bias=T.BB[:, b:b + 1],
                                          scale=1.0)))
        else:
            if not waited:
                V.wait_ge(sem.v, kb)
                waited = True
            ku = v(V.tensor_scalar(us, T.RA[:, 0:AW + 1], T.EF[:, b:b + 1], 2.0, A.is_gt, A.mult))
            ks = (sem.v, v(V.tensor_scalar(sb, T.NR[:], T.BB[:, b:b + 1], 0.5, A.is_lt, A.subtract)))
        ready[b] = [(sem.v, ku), ks]
    for b in order:
        for q, n in ready[b]:
            PE.wait_ge(q, n)
        kp = t(PE.matmul(T.psP[:, 0:AW + 1], T.S[:, b, :], T.U[:, US * b:US * b + AW + 1], b == order[0],
                         b == order[-1]))
    V.wait_ge(sem.t, kp)
    k = v(V.tensor_copy(T.PT[:, 0:AW + 1], T.psP[:, 0:AW + 1]))
    PE.wait_ge(sem.v, k)
    for h in range(NH):
        cs = slice(128 * h, 128 * h + 128)
        po = T["psO%d" % h]
        t(PE.matmul(po[:, 0:AW], T.CA[:, cs], T.PT[:, 1:AW + 1], True, False))
        k = t(PE.matmul(po[:, 0:AW], T.CB[:, cs], T.PT[:, 0:AW], False, True))
        V.wait_ge(sem.t, k)
        vo = v(V.tensor_scalar(T.OFF[:, h:256:NH], po[:, 0:AW], 0.5, None, A.mult))

    for q, n in xwaits:
        V.wait_ge(q, n)
        SC.wait_ge(q, n)
    V.wait_ge(sem.v, vo)
    SC.wait_ge(sem.v, vo)
    win = T.W[:, 0:zc + 4]
    c = 0
    pieces = []
    for w in CH:
        d = c + w
        kv = v(V.tensor_copy(T.Y[:, c:d], win.indirect(T.OFF[:, c // 16:d // 16])))
        k2 = sc(SC.activation(T.Y[:, d:d + w], win.indirect(T.OFF[:, d // 16:(d + w) // 16]),
                              ActivationFunctionType.Copy))
        pieces.append((kv, k2, c, 2 * w))
        c += 2 * w
    for kv, k2, c, w in pieces:
        g.sync.wait_ge(sem.v, kv)
        g.sync.wait_ge(sem.s, k2)
        g.sync.dma_start(T.y[:, c:c + w], T.Y[:, c:c + w]).then_inc(sem.ys, 16)
    g.sync.wait_ge(sem.ys, 16 * len(pieces))
